import numpy as np
import ml_dtypes


def mxq(x, axis, fmt="e4m3"):
    dtype, down = {"e4m3": (ml_dtypes.float8_e4m3fn, 7), "e5m2": (ml_dtypes.float8_e5m2, 14)}[fmt]
    v = np.moveaxis(np.asarray(x, np.float32).astype(ml_dtypes.bfloat16).astype(np.float64), axis, -1)
    blocks = v.reshape(v.shape[:-1] + (-1, 32))
    amax = np.abs(blocks).max(-1, keepdims=True)
    byte = np.maximum(np.where(amax > 0, np.frexp(amax)[1] - 1 + 127, 0) - down, 1)
    scale = np.exp2(byte - 127.0)
    codes = (blocks / scale).astype(np.float32).astype(dtype).astype(np.float64)
    return np.moveaxis((codes * scale).reshape(v.shape), -1, axis)


WIDE = False


def mx_kscale(k):
    if not WIDE:
        return np.ones(k)
    levels = np.array([10, -10, 5, -5, 0])
    if k % 512:
        return np.exp2(np.random.permutation(np.resize(levels, k // 32))).repeat(32)
    a = np.empty((k // 512, 16))
    for p in range(k // 512):
        a[p, :8] = np.random.permutation(np.resize(levels, 8))
        for g in range(8):
            far = levels[np.abs(levels - a[p, g]) >= 10]
            a[p, g + 8] = far[np.random.randint(len(far))]
    return np.exp2(a.ravel()).repeat(32)


BF16 = ml_dtypes.bfloat16


def bf(x):
    return np.asarray(x, np.float32).astype(BF16)


def f64(x):
    return np.asarray(x).astype(np.float64)

def planes(Y):
    n, m = Y.shape
    b = f64(bf(Y)).reshape(n // 32, 32, m)
    amax = np.abs(b).max(1)
    byte = np.clip(np.where(amax > 0, np.frexp(amax)[1] - 1 + 127 - 7, 1), 1, 254)
    codes = (b * np.exp2(127.0 - byte)[:, None, :]).reshape(n, m).astype(np.float32).astype(ml_dtypes.float8_e4m3fn).view(np.uint8)
    words = codes.reshape(n // 512, 128, 4, m).transpose(0, 1, 3, 2)
    return np.ascontiguousarray(words), np.ascontiguousarray(byte.astype(np.uint8).reshape(n // 512, 16, m))


B, K2, N = 1024, 1024, 2048


def sigmoid(v):
    return 1.0 / (1.0 + np.exp(-v))


def split_complex(x):
    half = x.shape[-1] // 2
    return x[:, :half], x[:, half:]


def setup_inputs():
    s, u = mx_kscale(K2), mx_kscale(N)
    return {"h": bf(np.random.standard_normal((B, K2))),
            "r": bf(np.random.standard_normal((B, K2))),
            "e": bf(np.random.standard_normal((N, K2)) / np.sqrt(K2) / s[None, :] / u[:, None]),
            "w": bf((1.0 + 0.1 * np.random.standard_normal(K2)) * s),
            "t": bf((1.0 + 0.1 * np.random.standard_normal(N)) * u),
            "y": bf(np.random.uniform(0.0, 1.0, (B, N)))}


def core(h, r, e, w, t, y):
    h, r, e, w, t, y = f64(h), f64(r), f64(e), f64(w), f64(t), f64(y)
    hr, hi = split_complex(h)
    rr, ri = split_complex(r)

    q = np.concatenate([hr * rr - hi * ri, hr * ri + hi * rr], axis=-1) * w[None, :]

    s = (mxq(q, 1, "e4m3") @ mxq(e, 1, "e4m3").T) * t[None, :]

    g = (sigmoid(s) - y) * t[None, :]

    dq = (mxq(g, 1, "e4m3") @ mxq(e, 0, "e4m3")) * w[None, :]
    dqr, dqi = split_complex(dq)

    return np.concatenate([dqr * rr + dqi * ri, dqi * rr - dqr * ri], axis=-1)


def reference(h, r, e, w, t, y):
    R_out = core(h, r, e, w, t, y)
    words, scales = planes(R_out.T)
    return R_out, words, scales

from contextlib import ExitStack

import concourse.mybir as mybir
from concourse.masks import make_identity

F32 = mybir.dt.float32
BF16 = mybir.dt.bfloat16
U32 = mybir.dt.uint32
I32 = mybir.dt.int32
U8 = mybir.dt.uint8
FP8X4 = mybir.dt.float8_e4m3fn_x4
ACT = mybir.ActivationFunctionType
ALU = mybir.AluOpType

P = 128
B, K, N = 1024, 1024, 2048
KG, NG, NQ = 2, 4, 4
QB = 256
FLOPS = 2 * 2 * B * K * N


def tile_complexonevsallgradient_x1_kernel(tc, h, r, e, w, t, y, out_0, out_1, out_2):
    nc = tc.nc
    V, G = nc.vector, nc.gpsimd
    with ExitStack() as ctx:
        keep = ctx.enter_context(tc.tile_pool(name="keep", bufs=1))
        nat = ctx.enter_context(tc.tile_pool(name="nat", bufs=4))
        big = ctx.enter_context(tc.tile_pool(name="big", bufs=3))
        mid = ctx.enter_context(tc.tile_pool(name="mid", bufs=2))
        sp = ctx.enter_context(tc.tile_pool(name="sp", bufs=2))
        ps = ctx.enter_context(tc.psum_pool(name="ps", bufs=2))
        ctx.enter_context(tc.manual_schedule())

        def bank(tag, bufs):
            return ps.tile([P, 512], F32, tag=tag, bufs=bufs, name=tag)

        t_bf = keep.tile([P, NG, 4], BF16, name="t_bf")
        w_bf = keep.tile([P, KG, 4], BF16, name="w_bf")
        t_f = keep.tile([P, NG, 4], F32, name="t_f")
        w_f = keep.tile([P, KG, 4], F32, name="w_f")
        ident = keep.tile([P, P], F32, name="ident")
        warm = keep.tile([P, 1], F32, name="warm")

        rT = keep.tile([P, KG, 2, B], F32, name="rT", align_bytes=64)
        qc = keep.tile([P, NQ, KG, QB], U32, name="qc", align_bytes=64)
        qs = keep.tile([P, NQ, KG, QB], U8, name="qs", align_bytes=64)
        ekc = keep.tile([P, NG, KG, 512], U32, name="ekc", align_bytes=64)
        eks = keep.tile([P, NG, KG, 512], U8, name="eks", align_bytes=64)
        enc = keep.tile([P, NG, 1024], U32, name="enc", align_bytes=64)
        ens = keep.tile([P, NG, 1024], U8, name="ens", align_bytes=64)
        gc = keep.tile([P, NG, B], U32, name="gc", align_bytes=64)
        gs = keep.tile([P, NG, B], U8, name="gs", align_bytes=64)
        rTb = rT[:].bitcast(BF16)

        make_identity(nc, ident[:])
        nc.vector.memset(warm[:], 0.0)
        nc.scalar.activation(out=warm[:], in_=warm[:], func=ACT.Sigmoid)

        r_n, h_n, e_n, y_n = {}, {}, {}, {}

        def load_rh(dst, src, q):
            dst[q] = nat.tile([P, 2, 1024], BF16, tag="rh", name="rh", bufs=4, align_bytes=64)
            nc.sync.dma_start(out=dst[q][:], in_=src[QB * q : QB * q + QB, :].rearrange("(i p) k -> p i k", p=P))

        def load_e(ng):
            e_n[ng] = nat.tile([P, 4, 1024], BF16, tag="e", name="e", bufs=3, align_bytes=64)
            nc.sync.dma_start(out=e_n[ng][:], in_=e[512 * ng : 512 * ng + 512, :].rearrange("(p j) k -> p j k", j=4))

        def load_y(q, nh):
            y_n[q, nh] = nat.tile([P, 2, 1024], BF16, tag="y", name="y", bufs=3, align_bytes=64)
            nc.sync.dma_start(out=y_n[q, nh][:], in_=y[QB * q : QB * q + QB, 1024 * nh : 1024 * nh + 1024].rearrange("(i p) n -> p i n", p=P))

        load_rh(r_n, r, 0)
        nc.sync.dma_start(out=w_bf[:], in_=w.rearrange("(g p j) -> p g j", p=P, j=4))
        load_rh(h_n, h, 0)
        load_e(0)
        nc.sync.dma_start(out=t_bf[:], in_=t.rearrange("(g p j) -> p g j", p=P, j=4))
        load_e(1)
        load_rh(r_n, r, 1)
        load_rh(h_n, h, 1)
        load_y(0, 0)
        load_e(2)
        load_y(0, 1)
        load_y(1, 0)
        rh_todo = [(dst, src, q) for q in (2, 3) for dst, src in ((r_n, r), (h_n, h))]
        y_todo = [(1, 1), (2, 0), (2, 1), (3, 0), (3, 1)]

        def next_rh():
            if rh_todo:
                load_rh(*rh_todo.pop(0))

        def next_y():
            if y_todo:
                load_y(*y_todo.pop(0))

        V.tensor_copy(out=w_f[:], in_=w_bf[:])
        G.tensor_copy(out=t_f[:], in_=t_bf[:])

        def words(tl, i, lo, u):
            return tl[:, i, :].bitcast(F32)[:, lo + u : lo + 256 : 2]

        def rview(u, el, q):
            return rTb[:, :, u, 2 * QB * q + el : 2 * QB * (q + 1) : 2]

        def rview_swapped(u, el, q):
            return rTb[:, ::-1, u, 2 * QB * q + el : 2 * QB * (q + 1) : 2]

        def pairs(ap):
            return ap.rearrange("p j (c i) -> p c j i", i=2)

        def outpairs(ap):
            return ap.rearrange("p (c i) j -> p c j i", i=2)

        live = {}

        def two_pairs(bk, tl, u):
            for g in range(KG):
                for i in range(2):
                    lo = QB * g + P * i
                    nc.tensor.transpose(bk[:, lo : lo + P], words(tl, i, 256 * g, u), ident[:])

        def r_front(q):
            for u in range(2):
                bk = bank("d", 3)
                two_pairs(bk, r_n[q], u)
                (V.tensor_copy if q in (0,) else nc.scalar.copy)(out=rT[:, :, u, QB * q : QB * q + QB], in_=bk[:].rearrange("p (g b) -> p g b", g=2))
            next_rh()

        def h_front(q, u):
            live["h", q, u] = bank("d", 3)
            two_pairs(live["h", q, u], h_n[q], u)
            if u == 1:
                next_rh()

        def h_prod(q, u):
            if u == 0:
                live["pr", q] = big.tile([P, 2, 4, QB], F32, tag="big", name="pr", align_bytes=64)
                live["pi", q] = big.tile([P, 2, 4, QB], F32, tag="big", name="pi", align_bytes=64)
            hv = live["h", q, u][:].rearrange("p (g b) -> p g b", g=2).bitcast(BF16)
            for el in range(2):
                j = 2 * u + el
                V.scalar_tensor_tensor(
                    out=live["pr", q][:, :, j, :], in0=hv[:, :, el::2], scalar=w_f[:, 0, j : j + 1],
                    in1=rview(u, el, q), op0=ALU.mult, op1=ALU.mult)
                V.scalar_tensor_tensor(
                    out=live["pi", q][:, :, j, :], in0=hv[:, :, el::2], scalar=w_f[:, 1, j : j + 1],
                    in1=rview_swapped(u, el, q), op0=ALU.mult, op1=ALU.mult)

        def h_add(q, g):
            if g == 0:
                live["qb", q] = mid.tile([P, 2, QB, 4], BF16, tag="qb", name="qb", bufs=2, align_bytes=64)
            eng, n = (V, QB) if (q, g) in ((0, 0), (0, 1), (1, 0), (1, 1), (2, 0), (2, 1), (3, 0),) else (G, QB // 2)
            nm, op = (("pr", ALU.subtract), ("pi", ALU.add))[g]
            pt = live[nm, q]
            for lo in range(0, QB, n):
                eng.tensor_tensor(out=outpairs(live["qb", q][:, g, lo : lo + n]), in0=pairs(pt[:, 0, :, lo : lo + n]), in1=pairs(pt[:, 1, :, lo : lo + n]), op=op)

        def h_quant(q):
            V.quantize_mx(out=qc[:, q].rearrange("p g b -> p (g b)").bitcast(FP8X4), scales=qs[:, q].rearrange("p g b -> p (g b)"),
                          in_=live["qb", q][:].rearrange("p g b j -> p (g b j)"))

        def ek_front(ng, g):
            live["kb", ng, g] = mid.tile([P, 512, 4], BF16, tag="kb", name="kb", bufs=3, align_bytes=64)
            kw = live["kb", ng, g][:].rearrange("p c j -> p (c j)").bitcast(F32)
            for hf in range(2):
                bk = bank("tr", 3)
                for u in range(2):
                    for i in range(2):
                        lo = 256 * u + P * i
                        nc.tensor.transpose(bk[:, lo : lo + P], words(e_n[ng], 2 * hf + i, 256 * g, u), ident[:])
                (V.tensor_copy if (ng, g) in () else nc.scalar.copy)(out=kw[:, 512 * hf : 512 * hf + 512].rearrange("p (c u) -> p c u", u=2),
                               in_=bk[:].rearrange("p (u c) -> p c u", u=2))

        def ek_quant(ng, g):
            V.quantize_mx(out=ekc[:, ng, g, :].bitcast(FP8X4), scales=eks[:, ng, g, :],
                          in_=live["kb", ng, g][:].rearrange("p c j -> p (c j)"))

        def g_copy(out, in_):
            G.tensor_scalar(out=out, in0=in_, scalar1=1.0, scalar2=0.0, op0=ALU.mult, op1=ALU.add)

        def en_copy(ng, g):
            live["nb", ng, g] = mid.tile([P, 512, 4], BF16, tag="kb", name="nb", bufs=3, align_bytes=64)
            copy = g_copy if (ng, g) in ((1, 0), (3, 1),) else V.tensor_copy if (ng, g) in () else nc.scalar.copy
            out = live["nb", ng, g][:].rearrange("p (j m) i -> p m j i", j=4)
            in_ = e_n[ng][:, :, 512 * g : 512 * g + 512].rearrange("p i (m j) -> p m j i", j=4)
            n = P // 2 if (ng, g) in ((1, 0), (3, 1),) else P
            for lo in range(0, P, n):
                copy(out=out[:, lo : lo + n], in_=in_[:, lo : lo + n])
            if (ng, g) == (0, 1):
                load_e(3)

        def en_quant(ng, g):
            cols = slice(512 * g, 512 * g + 512)
            V.quantize_mx(out=enc[:, ng, cols].bitcast(FP8X4), scales=ens[:, ng, cols],
                          in_=live["nb", ng, g][:].rearrange("p c i -> p (c i)"))

        def u_heavy(q, ng):
            return (q, ng) in ((0, 0), (0, 2), (0, 3), (1, 2), (1, 3), (2, 0), (2, 2), (3, 1), (3, 2), (3, 3),)

        def u_front(q, ng):
            cols = slice(QB * q, QB * q + QB)
            yb = bank("tr", 3)
            for u in range(2):
                for i in range(2):
                    lo = QB * u + P * i
                    nc.tensor.transpose(yb[:, lo : lo + P], words(y_n[q, ng // 2], i, 256 * (ng % 2), u), ident[:])
            if ng % 2 == 1:
                next_y()
            sig = sp.tile([P, 4, QB], F32, tag="sig", name="sig", bufs=3, align_bytes=64)
            for u in range(2):
                acc = bank("s", 2)
                for el in range(2):
                    j = 2 * u + el
                    ac = acc[:, QB * el : QB * el + QB]
                    for g in range(KG):
                        nc.tensor.matmul_mx(
                            out=ac, lhsT=ekc[:, ng, g, P * j : P * j + P].bitcast(FP8X4), lhsT_scale=eks[:, ng, g, P * j : P * j + P],
                            rhs=qc[:, q, g, :].bitcast(FP8X4), rhs_scale=qs[:, q, g, :], start=(g == 0), stop=(g == KG - 1))
                for el in range(2):
                    j = 2 * u + el
                    nc.scalar.activation(out=sig[:, j, :], in_=acc[:, QB * el : QB * el + QB], func=ACT.Sigmoid, scale=t_f[:, ng, j : j + 1])
            live["sig", q, ng], live["yb", q, ng] = sig, yb

        def u_diff(q, ng):
            sig = live["sig", q, ng]
            yv = live["yb", q, ng][:].bitcast(BF16).rearrange("p (u b x) -> p u x b", u=2, x=2)
            live["dt", q, ng] = sp.tile([P, 4, QB], F32, tag="dt", name="dt", bufs=2, align_bytes=64)
            dt = live["dt", q, ng]
            if u_heavy(q, ng):
                for j in range(4):
                    nc.scalar.activation(out=dt[:, j, :], in_=yv[:, j // 2, j % 2, :], func=ACT.Copy, scale=t_f[:, ng, j : j + 1])
                for j in range(4):
                    nc.scalar.activation(out=sig[:, j, :], in_=sig[:, j, :], func=ACT.Copy, scale=t_f[:, ng, j : j + 1])
            else:
                V.tensor_tensor(out=dt[:].rearrange("p (u x) b -> p u x b", u=2), in0=sig[:].rearrange("p (u x) b -> p u x b", u=2), in1=yv, op=ALU.subtract)

        def u_g(q, ng):
            live["gb", q, ng] = mid.tile([P, QB, 4], BF16, tag="gb", name="gb", bufs=2, align_bytes=64)
            gview = outpairs(live["gb", q, ng][:])
            if u_heavy(q, ng):
                V.tensor_tensor(out=gview, in0=pairs(live["sig", q, ng][:]), in1=pairs(live["dt", q, ng][:]), op=ALU.subtract)
            else:
                eng, n = (G, QB // 2) if (q, ng) in ((0, 1), (1, 0), (3, 0),) else (V, QB)
                for lo in range(0, QB, n):
                    eng.tensor_tensor(out=outpairs(live["gb", q, ng][:, lo : lo + n]), in0=pairs(live["dt", q, ng][:, :, lo : lo + n]),
                                      in1=t_f[:, ng, :].unsqueeze(1).unsqueeze(3).to_broadcast([P, n // 2, 4, 2]), op=ALU.mult)

        def u_quant(q, ng):
            cols = slice(QB * q, QB * q + QB)
            V.quantize_mx(out=gc[:, ng, cols].bitcast(FP8X4), scales=gs[:, ng, cols],
                          in_=live["gb", q, ng][:].rearrange("p b j -> p (b j)"))

        def w_front(q, j):
            cols = slice(QB * q, QB * q + QB)
            bk = bank("d", 3)
            for g in range(KG):
                for ng in range(NG):
                    lo = 512 * g + P * j
                    nc.tensor.matmul_mx(
                        out=bk[:, QB * g : QB * g + QB], lhsT=enc[:, ng, lo : lo + P].bitcast(FP8X4), lhsT_scale=ens[:, ng, lo : lo + P],
                        rhs=gc[:, ng, cols].bitcast(FP8X4), rhs_scale=gs[:, ng, cols], start=(ng == 0), stop=(ng == NG - 1))
            live["w", q, j] = bk

        def w_prod(q, j):
            if j == 0:
                live["o", q] = big.tile([P, 2, 4, QB], F32, tag="big", name="ot", align_bytes=64)
            if j % 2 == 0:
                live["at", q, j // 2] = sp.tile([P, 2, 2, QB], F32, tag="at", name="at", bufs=2, align_bytes=64)
                live["bt", q, j // 2] = sp.tile([P, 2, 2, QB], F32, tag="bt", name="bt", bufs=2, align_bytes=64)
            bk = live["w", q, j]
            for g, nm in enumerate(("at", "bt")):
                V.scalar_tensor_tensor(
                    out=live[nm, q, j // 2][:, j % 2], in0=bk[:, QB * g : QB * g + QB].unsqueeze(1).to_broadcast([P, 2, QB]), scalar=w_f[:, g, j : j + 1],
                    in1=rview(j // 2, j % 2, q), op0=ALU.mult, op1=ALU.mult)

        def w_add(q, u, g):
            eng = V if (q, u, g) in ((0, 1, 0), (1, 0, 0), (2, 1, 0), (3, 0, 0), (3, 1, 0), (3, 1, 1),) else G
            at, bt, ot = live["at", q, u], live["bt", q, u], live["o", q]
            if g == 0:
                eng.tensor_tensor(out=ot[:, 0, 2 * u : 2 * u + 2, :], in0=at[:, :, 0, :], in1=bt[:, :, 1, :], op=ALU.add)
            else:
                eng.tensor_tensor(out=ot[:, 1, 2 * u : 2 * u + 2, :], in0=bt[:, :, 0, :], in1=at[:, :, 1, :], op=ALU.subtract)

        def o_cast(q):
            live["ob", q] = mid.tile([P, 2, QB, 4], BF16, tag="qb", name="ob", bufs=2, align_bytes=64)
            for g in range(KG):
                copy = g_copy if (q, g) in () else V.tensor_copy if (q, g) in ((3, 0), (3, 1),) else nc.scalar.copy
                copy(out=outpairs(live["ob", q][:, g]), in_=pairs(live["o", q][:, g]))

        def o_rows(q, i):
            row = mid.tile([P, 1024], F32, tag="row", name="row", bufs=2, align_bytes=64)
            for g in range(KG):
                bk = bank("tr", 3)
                for j in range(4):
                    nc.tensor.transpose(bk[:, P * j : P * j + P], live["o", q][:, g, j, P * i : P * i + P], ident[:])
                (V.tensor_copy if (q, i) in ((0, 1),) else nc.scalar.copy)(out=row[:, 512 * g : 512 * g + 512].rearrange("p (m j) -> p m j", j=4),
                               in_=bk[:].rearrange("p (j m) -> p m j", j=4))
            b0 = QB * q + P * i
            nc.sync.dma_start(out=out_0[b0 : b0 + P, :], in_=row[:])

        def o_quant(q):
            oc = sp.tile([P, 2, QB], U32, tag="oc", name="oc", bufs=2, align_bytes=64)
            osc = sp.tile([P, 2, QB], U8, tag="osc", name="osc", bufs=2, align_bytes=64)
            cols = slice(QB * q, QB * q + QB)
            V.quantize_mx(out=oc[:].rearrange("p g b -> p (g b)").bitcast(FP8X4), scales=osc[:].rearrange("p g b -> p (g b)"),
                          in_=live["ob", q][:].rearrange("p g b j -> p (g b j)"))
            for g in range(KG):
                nc.sync.dma_start(out=out_1[g, :, cols, :].rearrange("p m i -> p (m i)").bitcast(I32), in_=oc[:, g, :].bitcast(I32))
            for qd in range(4):
                nc.sync.dma_start(out=out_2[:, 4 * qd : 4 * qd + 4, cols].rearrange("g q m -> q g m").bitcast(I32),
                                  in_=osc[32 * qd : 32 * qd + 4, :, :].bitcast(I32))

        def R(q):
            return [(0, lambda: r_front(q))]

        def H(q, u):
            parts = [(0, lambda: h_front(q, u)), (1 if u == 0 else 0, lambda: h_prod(q, u))]
            if u == 1:
                parts += [(2, lambda: h_add(q, 0)), (5, lambda: h_add(q, 1)), (7, lambda: h_quant(q))]
            return parts

        def EK(ng, g):
            return [(0, lambda: ek_front(ng, g)), (2, lambda: ek_quant(ng, g))]

        def EN(ng, g):
            return [(0, lambda: en_copy(ng, g)), (1, lambda: en_quant(ng, g))]

        def U(q, ng):
            return [(0, lambda: u_front(q, ng)), (1, lambda: u_diff(q, ng)), (3, lambda: u_g(q, ng)), (5, lambda: u_quant(q, ng))]

        def W(q, j):
            parts = [(0, lambda: w_front(q, j)), ((1, 0, 1, 1)[j], lambda: w_prod(q, j))]
            if j % 2 == 1:
                parts += [(4 if j == 1 else 2, lambda: w_add(q, j // 2, 0)), (2 if j == 1 else 2, lambda: w_add(q, j // 2, 1))]
            if j == 3:
                parts += [(5, lambda: o_cast(q)), (5, lambda: o_rows(q, 0)), (6, lambda: o_rows(q, 1)), (8, lambda: o_quant(q))]
            return parts

        order = [R(0), H(0, 0), H(0, 1), EN(0, 0), EK(0, 0), EK(0, 1), EK(1, 1), EK(1, 0), R(1), H(1, 0), H(1, 1), EN(1, 0), EN(0, 1), U(0, 0), EK(2, 1), EN(2, 0), EK(2, 0), U(0, 1), R(2), H(2, 0), U(1, 0), EN(1, 1), H(2, 1), EK(3, 0), EN(3, 0), EK(3, 1), U(0, 2), R(3), H(3, 0), U(1, 2), H(3, 1), U(0, 3), EN(3, 1), U(1, 1), U(2, 3), EN(2, 1), U(1, 3), W(0, 0), U(2, 0), W(0, 1), W(0, 2), U(2, 2), W(0, 3), U(2, 1), U(3, 0), W(1, 0), W(1, 2), U(3, 1), W(1, 1), U(3, 2), W(1, 3), U(3, 3), W(2, 0), W(2, 1), W(2, 2), W(2, 3), W(3, 0), W(3, 1), W(3, 2), W(3, 3)]
        pend = {}
        for s in range(len(order) + 10):
            if s < len(order):
                for lag, fn in order[s]:
                    pend.setdefault(s + lag, []).append((-lag, fn))
            for item in sorted(pend.get(s, []), key=lambda x: x[0]):
                item[1]()
